import numpy as np, ml_dtypes
CORES = [3,7,11,15,131,135,139,143]
N = 8
import mx_ref
BF = ml_dtypes.bfloat16
def gentries(a):
    return np.ascontiguousarray(a.reshape(8, 16, -1).transpose(0, 2, 1)).reshape(8, -1)
def gtable(e):
    e = np.asarray(e); return np.ascontiguousarray(e.reshape(8, -1, 16).transpose(0, 2, 1)).reshape(128, -1).astype(np.int32)
def gcols(t, e):
    v = np.concatenate([t.reshape(8, 16, -1, 4), np.zeros((8, 16, 1, 4), BF)], axis=2)
    return np.ascontiguousarray(np.stack([v[g][:, e[g]] for g in range(8)])).reshape(128, -1)
def tile(rs):
    return np.stack(rs, axis=2).reshape(128, -1).astype(BF)
def pick(q, e):
    c = np.concatenate([q[0].reshape(128, -1, 4), np.zeros((128, 1, 4), np.uint8)], axis=1); s = np.concatenate([q[1], np.ones((16, 1), np.uint8)], axis=1)
    return (np.ascontiguousarray(c[:, e].reshape(128, -1)), np.ascontiguousarray(s[:, e]))
def join(*qs):
    return (np.concatenate([q[0] for q in qs], axis=1), np.concatenate([q[1] for q in qs], axis=1))
def put(q, e, v):
    c, s = q[0].reshape(128, -1, 4).copy(), q[1].copy(); c[:, e] = v[0].reshape(128, -1, 4); s[:, e] = v[1]
    return (c.reshape(128, -1), s)
def pk(c, s):
    return (np.ascontiguousarray(c), mx_ref.live(s))
def emit(q):
    return q[0], q[1]
def packed(v, rng):
    q = [mx_ref.quantize(np.ascontiguousarray(v[r])) for r in range(N)]
    return np.stack([a for a, b in q]), np.stack([mx_ref.plane(b, rng) for a, b in q])
def f(rng, *shape):
    return mx_ref.flush((rng.standard_normal(shape, dtype=np.float32) * np.exp2(rng.integers(-2, 3, shape[:-1] + (1,)))).astype(BF))
def wide(rng, *shape, cols=0):
    v = rng.standard_normal(shape, dtype=np.float32) * np.exp2(rng.integers(-12, 13, shape)).astype(np.float32)
    if cols: v *= np.repeat(np.exp2(rng.integers(-cols, cols + 1, shape[:-2] + (1, shape[-1] // 4))) * (rng.random(shape[:-2] + (1, shape[-1] // 4)) > 0.0625), 4, axis=-1).astype(np.float32)
    return mx_ref.flush(v.astype(BF))
C, R = 384, 2
def partners(rng, n):
    e = np.tile(np.arange(C), (N, 8, 1))
    p = rng.permuted(e, axis=2)
    k, m = p[:, :, :n], p[:, :, n:2 * n]
    np.put_along_axis(e, k, m, axis=2)
    np.put_along_axis(e, m, k, axis=2)
    return e
def stored(e):
    return np.stack([gtable(e[r]) for r in range(N)])
def layers(rng, v, w):
    (a, b), (c, d) = packed(v, rng), packed(w, rng)
    return {"vc": a, "vs": b, "wc": c, "ws": d}
def units(rng, kv, kw):
    w = np.zeros((N, 128, 4, 128, 4), np.float32)
    i = np.arange(128)
    for b in range(4): w[:, i, b, i, b] = 1
    w = w.reshape(N, 128, 2048)
    return layers(rng, *[(w * np.reshape(k, (N, 1, 1)).astype(np.float32) + np.float32(0.0)).astype(BF) for k in (kv, kw)])
def moves_alone(rng):
    k = rng.permutation(N) % 2 * 32.0
    return units(rng, k, 32.0 - k)
def setup_inputs(rng):
    return {"x": np.array(f(rng, N, 128, 4 * C)), "pr": stored(partners(rng, int(rng.integers(3 * C // 8, C // 2 + 1)))), "u": np.array(f(rng, N, 128, 512)), "a": np.array(f(rng, N, 128, 512)), **layers(rng, f(rng, N, 128, 2048), f(rng, N, 128, 2048))}
def setup_inputs_rest(rng):
    d = setup_inputs(rng)
    e = partners(rng, C // 2)
    o = rng.permutation(N)
    d["x"][o[0]] = 0
    e[o[1]] = np.arange(C)
    d["pr"] = stored(e)
    return d
def setup_inputs_near(rng):
    d = setup_inputs(rng)
    e = partners(rng, C // 2)
    j = np.arange(C)
    n = np.cumsum(e > j, axis=2) - 1
    n = np.take_along_axis(n, np.minimum(e, j), axis=2)
    flip = np.take_along_axis(rng.integers(0, 2, (N, 8, C // 2)), n, axis=2) > 0
    h = np.take_along_axis(rng.integers(-3, 4, (N, 8, C // 2)), n, axis=2)
    first = (e > j) ^ flip
    kind = n % 9
    plus = np.where(kind == 7, True, np.where(kind == 8, False, first))
    m = np.where(first, h, kind - 3 - h)
    size = np.exp2(np.arange(4) - 23.0)
    x = np.zeros((N, 8, 16, C, 4), np.float32)
    x[:, :, 0, :, 0] = plus
    x[:, :, 1, :, 0] = ~plus
    x[:, :, 2:8] = rng.integers(4, 8, (N, 8, 6, C, 4)) * 0.125
    x[:, :, 8] = ((np.maximum(m, 0)[..., None] >> np.arange(4)) & 1) * size
    x[:, :, 9] = ((np.maximum(-m, 0)[..., None] >> np.arange(4)) & 1) * size
    x[:, :, 10:] = rng.integers(4, 8, (N, 8, 6, C, 4)) * 2.0 ** -20
    u = np.zeros((N, 128, 8, 4), np.float32)
    for g in range(8):
        u[:, 16 * g, g, 0] = 1
        u[:, 16 * g + 1, g, 0] = -1
        u[:, 16 * g + 8, g] = 1
        u[:, 16 * g + 9, g] = -1
    z = rng.permutation(N) % 3 - 1.0
    x = x * np.exp2(7 * z).reshape(N, 1, 1, 1, 1)
    u = u * np.exp2(30 * z).reshape(N, 1, 1, 1) + 0.0
    d["x"] = x.astype(np.float32).reshape(N, 128, 4 * C).astype(BF)
    d["pr"] = stored(e)
    d["u"].reshape(N, 128, 128, 4)[:, :, ::16] = u.astype(np.float32).astype(BF)
    return {**d, **moves_alone(rng)}
def setup_inputs_huge(rng):
    d = setup_inputs(rng)
    x = 2.0 ** 30 * (0.6 + 0.4 * rng.random((N, 128, C, 4)))
    s = np.stack([rng.permutation(8) % 2 * 2.0 - 1.0 for r in range(N)])
    o = rng.permutation(N)
    s[o[0]] = 1
    s[o[1]] = -1
    g = np.ones((N, 128, 8)) * s[:, None, :]
    for r in o[2::2]:
        g[r, 64:] *= -1
        c = rng.permutation(C) % 2 == 0
        x[r, :64] *= np.where(c, 1.0, 2.0 ** -20)[None, :, None]
        x[r, 64:] *= np.where(c, 2.0 ** -20, 1.0)[None, :, None]
    u = 2.0 ** 30 * (1 - 0.25 * rng.random((N, 128, 8, 4))) * g[..., None]
    d["x"] = x.astype(np.float32).reshape(N, 128, 4 * C).astype(BF)
    d["pr"] = stored(partners(rng, C // 2))
    d["u"].reshape(N, 128, 128, 4)[:, :, ::16] = u.astype(np.float32).astype(BF)
    return {**d, **moves_alone(rng)}
def setup_inputs_flip(rng):
    d = setup_inputs(rng)
    x = (1 + rng.random((N, 128, C, 4))) * np.exp2(rng.integers(24, 29, (N, 1, C, 1)))
    u = (1 + rng.random((N, 128, 8, 4))) * (rng.permutation(N) % 2 * 2.0 - 1.0).reshape(N, 1, 1, 1)
    d["x"] = x.astype(np.float32).reshape(N, 128, 4 * C).astype(BF)
    d["pr"] = stored(partners(rng, C // 2))
    d["u"].reshape(N, 128, 128, 4)[:, :, ::16] = u.astype(np.float32).astype(BF)
    return {**d, **units(rng, np.full(N, -32.0), np.full(N, -32.0))}
def setup_inputs_spread(rng):
    d = setup_inputs(rng)
    d["x"] = wide(rng, N, 128, 4 * C, cols=6)
    return d
def check_inputs(d):
    b = []
    for k in ("x", "u", "a"):
        v = np.abs(d[k].astype(np.float32))
        if not (np.isfinite(v).all() and ((v == 0) | (v >= 2.0 ** -30) & (v <= 2.0 ** 30)).all()): b.append("a value of " + k)
    e = np.stack([gentries(p) for p in d["pr"]])
    if ((e < 0) | (e >= C)).any(): b.append("an entry of pr is out of range")
    elif (np.take_along_axis(e, e, axis=2) != np.arange(C)).any(): b.append("a column isn't its partner's partner")
    for k in ("v", "w"):
        c = d[k + "c"] & 127
        s = np.stack([mx_ref.live(p) for p in d[k + "s"]]).astype(int)
        if (c == 127).any(): b.append("a code of " + k + "c isn't a number")
        full = c.reshape(N, 16, 8, 512, 4).any(axis=(2, 4))
        if ((s > 157) | full & (s < 80)).any(): b.append("a scale of " + k + "s is out of range")
    return b
def reference(x, pr, u, a, vc, vs, wc, ws):
    partner = [gentries(pr[r]) for r in range(N)]
    qu = [mx_ref.quantize(u[r]) for r in range(N)]
    lv, lw = [pk(vc[r], vs[r]) for r in range(N)], [pk(wc[r], ws[r]) for r in range(N)]
    four = [np.arange(128 * b, 128 * b + 128) for b in range(4)]
    now = [x[r] for r in range(N)]
    last = np.zeros((N, 8, C), int)
    for t in range(R):
        start = np.arange(C)
        q = []
        for r in range(N):
            s = mx_ref.matmul(qu[r], mx_ref.quantize(now[r]))[::16]
            c = np.where(s + np.take_along_axis(s, partner[r], axis=1) > 0, partner[r], np.arange(C))
            l = [c[0]]
            for g in range(1, 8): l.append(c[g][l[g - 1]])
            l = np.stack(l)
            last[r] = l[:, start]
            q.append(mx_ref.quantize(gcols(now[r], last[r])))
            start = l[7][start]
        now = [tile([np.maximum(mx_ref.matmul(pick(lv[r], k), q[r]), mx_ref.matmul(pick(lw[r], k), q[(r - 1) % N])) * np.float32(0.03125) for k in four]) for r in range(N)]
    y, ol = np.zeros((N, 128, C), np.float32), np.zeros((N, 8, C), np.float32)
    oc, osc = np.zeros((N, 128, 4 * C), np.uint8), np.zeros((N, 16, C), np.uint8)
    for r in range(N):
        z = mx_ref.quantize(now[r])
        y[r] = mx_ref.matmul(mx_ref.quantize(a[r]), z)
        ol[r] = last[r]
        oc[r], osc[r] = emit(z)
    return {"y": y, "ol": ol, "oc": oc, "osc": osc}

@@ -1,0 +1,490 @@
+from concourse.bass import DstId, RemoteDMATransfer
+from concourse.mybir import dt, AluOpType, ActivationFunctionType
+
+N, C, ROUNDS = 8, 384, 2
+H = C // 2
+K = C // 16
+MID = C // 2
+ROW = C + 16
+SCALE = 0.03125
+CODES, PLANE = "float8_e4m3fn_x4", "uint8"
+
+SCRATCH = {
+    "xt0": ("sbuf", [128, 4 * C], "bfloat16"), "xt1": ("sbuf", [128, 4 * C], "bfloat16"), "xt2": ("sbuf", [128, 4 * C], "bfloat16"),
+    "ut": ("sbuf", [128, 512], "bfloat16"), "at": ("sbuf", [128, 512], "bfloat16"),
+    "qu": ("sbuf", [128, 128], CODES), "su": ("sbuf", [128, 128], PLANE),
+    "qa": ("sbuf", [128, 128], CODES), "sa": ("sbuf", [128, 128], PLANE),
+    "qv": ("sbuf", [128, 512], CODES), "sv": ("sbuf", [128, 512], PLANE),
+    "qw": ("sbuf", [128, 512], CODES), "sw": ("sbuf", [128, 512], PLANE),
+    "pri": ("sbuf", [128, K], "int32"), "prw": ("sbuf", [128, K], "uint16"),
+    "pi": ("sbuf", [128, 4], "int32"), "pf": ("sbuf", [128, 12], "float32"),
+    "jw": ("sbuf", [128, K], "float32"), "iw": ("sbuf", [128, K], "float32"), "ew": ("sbuf", [128, 2], "float32"),
+    "xl": ("sbuf", [128, 6], "uint16"),
+    "idw": ("sbuf", [128, C], "bfloat16"),
+    "d0": ("sbuf", [128, 2 * C], "float16"), "d1": ("sbuf", [128, 2 * C], "bfloat16"),
+    "cc": ("sbuf", [128, 2 * C + 64], "bfloat16"),
+    "ww": ("sbuf", [128, 4 * ROW + 16], "bfloat16"), "ow": ("sbuf", [128, C], "bfloat16"),
+    "tt": ("sbuf", [128, 2 * ROW + K], "bfloat16"),
+    "ss": ("sbuf", [128, C], "float32"), "ns": ("sbuf", [128, C], "float32"),
+    "e1": ("sbuf", [128, 32], "uint16"), "eq": ("sbuf", [128, 32], "uint16"), "eo": ("sbuf", [128, 32], "uint16"),
+    "lq": ("sbuf", [128, 3 * K], "uint16"),
+    "pvs": ("sbuf", [128, 4 * C], "float32"),
+    "ys": ("sbuf", [128, C], "float32"), "ols": ("sbuf", [128, C], "float32"),
+    "ps": ("psum", [128, 8 * 512], "float32"),
+}
+for _t in range(ROUNDS + 1):
+    SCRATCH["qx%d" % _t] = ("sbuf", [128, C], CODES)
+    SCRATCH["sx%d" % _t] = ("sbuf", [128, C], PLANE)
+for _t in range(ROUNDS):
+    SCRATCH["pl%d" % _t] = ("sbuf", [128, 4 * C], "bfloat16")
+    SCRATCH["yt%d" % _t] = ("sbuf", [128, 4 * C], "bfloat16")
+    SCRATCH["mx%d" % _t] = ("sbuf", [128, 4 * C], "float32")
+    for _n in ("y", "z", "p"):
+        SCRATCH["q%s%d" % (_n, _t)] = ("sbuf", [128, C], CODES)
+        SCRATCH["s%s%d" % (_n, _t)] = ("sbuf", [128, C], PLANE)
+    SCRATCH["el%d" % _t] = ("sbuf", [128, 32], "uint16")
+    SCRATCH["eb%d" % _t] = ("sbuf", [128, 32], "uint16")
+    SCRATCH["ll%d" % _t] = ("sbuf", [128, (N - 1) * K], "uint16")
+
+SEMAPHORES = (["cv", "ca", "cp", "cg", "sent", "dx0", "dx1", "du", "dpr", "dvc", "dvs", "dwc", "dws", "da", "outs", "outa"]
+              + ["dat%d" % t for t in range(ROUNDS)] + ["lst%d_%d" % (t, s) for t in range(ROUNDS) for s in range(N - 1)])
+
+
+def _mask(engines):
+    m = 0
+    for e in engines:
+        m |= 1 << e
+    return m
+
+
+def _near(T, topo, a, b):
+    return T.cores[b] in topo.cores_of(T.cores[a])
+
+
+def _lanes(T, topo, r):
+    me = T.cores[r]
+    own = topo.cores_of(me)
+    far = topo.engines(me, [c for c in T.cores if c not in own][0])
+    near = [e for e in topo.engines(me, [c for c in own if c != me][0]) if e not in far]
+    return far, near
+
+
+def _list_dests(s):
+    if s == N - 1:
+        return []
+    return ([0] if s else []) + list(range(s + 1, N))
+
+
+def _data_engines(T, topo, r):
+    far, near = _lanes(T, topo, r)
+    if _near(T, topo, r, (r + 1) % N):
+        return [near, far + near, far + near]
+    return [far, far, far]
+
+
+def _list_engines(T, topo, s, d):
+    far, near = _lanes(T, topo, s)
+    return near if _near(T, topo, s, d) else far
+
+
+def rank_program(g, core, T, topo):
+    r = T.rank_of(core)
+    if r is None:
+        return
+    A, F = AluOpType, ActivationFunctionType
+    V, S, P = g.vector, g.scalar, g.tensor
+    queue = {"v": V, "a": S, "p": P, "g": g, "s": g.sync}
+    known = {q: {} for q in queue}
+    count, waited = {}, {}
+    writer, readers = {}, {}
+
+    def wait(q, ev):
+        sem, n, clock, _ = ev
+        if known[q].get(sem, 0) < n:
+            queue[q].wait_ge(T.sem[sem], n)
+            waited[sem] = max(waited.get(sem, 0), n)
+        for k, v in clock.items():
+            if known[q].get(k, 0) < v:
+                known[q][k] = v
+
+    def order(q, reads, writes):
+        deps = [writer[k] for k in reads + writes if k in writer]
+        for k in writes:
+            deps += readers.get(k, [])
+        for k in reads:
+            if k.startswith("ps"):
+                deps += [e for e in readers.get(k, []) if e[3] != q]
+        top = {}
+        for e in deps:
+            if e[0] not in top or top[e[0]][1] < e[1]:
+                top[e[0]] = e
+        for e in top.values():
+            wait(q, e)
+
+    def note(q, sem, inc, reads, writes):
+        count[sem] = count.get(sem, 0) + inc
+        clock = dict(known[q])
+        clock[sem] = count[sem]
+        ev = (sem, count[sem], clock, q)
+        for k in reads:
+            readers.setdefault(k, []).append(ev)
+        for k in writes:
+            writer[k] = ev
+            readers[k] = []
+
+    def op(q, fn, reads, writes):
+        order(q, reads, writes)
+        fn().then_inc(T.sem["c" + q], 1)
+        note(q, "c" + q, 1, reads, writes)
+
+    def dma(q, sem, out, in_, reads, writes):
+        order(q, reads, writes)
+        queue[q].dma_start(out, in_).then_inc(T.sem[sem], 16)
+        note(q, sem, 16, reads, writes)
+
+    def arrives(sem, n, keys):
+        count[sem] = n
+        for k in keys:
+            writer[k] = (sem, n, {sem: n}, "far")
+
+    def bank(b, n):
+        return T.ps[:, 512 * b:512 * b + n]
+
+    def ts(out, in0, s1, s2, o0, o1, reads, writes):
+        if o1 is None:
+            op("v", lambda: V.tensor_scalar(out, in0, s1, None, o0), reads, writes)
+        else:
+            op("v", lambda: V.tensor_scalar(out, in0, s1, s2, o0, o1), reads, writes)
+
+    def vcopy(out, in_, reads, writes):
+        op("v", lambda: V.tensor_copy(out, in_), reads, writes)
+
+    def acopy(out, in_, reads, writes, **kw):
+        f = F.Identity if "bias" in kw else F.Copy
+        op("a", lambda: S.activation(out, in_, f, **kw), reads, writes)
+
+    def quant(q, s, tile, lo, hi, reads, writes):
+        op("v", lambda: V.quantize_mx(q[:, lo:hi], s[:, lo:hi], tile[:, 4 * lo:4 * hi]), reads, writes)
+
+    def mm(b, lq, ls, l0, rq, rs, lo, hi, reads):
+        op("p", lambda: P.matmul_mx(bank(b, hi - lo), lq[:, l0:l0 + 128], ls[:, l0:l0 + 128], rq[:, lo:hi], rs[:, lo:hi], True, True),
+           reads, ["ps%d" % b])
+
+    def row(i):
+        return T.ww[:, ROW * i + 16:ROW * i + 16 + C]
+
+    def rowpart(i, lo, hi):
+        return T.ww[:, ROW * i + 16 + lo:ROW * i + 16 + hi]
+
+    def wk(i):
+        return ["w%d_0" % i, "w%d_1" % i]
+
+    def step(win, wkeys, lst, l0, lkeys, i, who="s"):
+        if who == "s":
+            vcopy(rowpart(i, 0, H), win.indirect(lst[:, l0:l0 + K // 2]), wkeys + lkeys, ["w%d_0" % i])
+            acopy(rowpart(i, H, C), win.indirect(lst[:, l0 + K // 2:l0 + K]), wkeys + lkeys, ["w%d_1" % i])
+        else:
+            (vcopy if who == "v" else acopy)(row(i), win.indirect(lst[:, l0:l0 + K]), wkeys + lkeys, wk(i))
+
+    def turn(a_in, b_in, reads):
+        op("v", lambda: V.transpose(T.tt[:, 0:C], a_in), reads, ["tta"])
+        op("v", lambda: V.transpose(T.tt[:, C:2 * ROW], b_in), reads + ["pads"], ["ttb"])
+
+    def turn_row(i):
+        turn(row(i), T.ww[:, ROW * i:ROW * i + C + 32], wk(i))
+
+    def take(out, x, key, mul=None, add=float(MID)):
+        win = T.tt[:, 0:2 * ROW + K].indirect(T.xl[:, 2 * x:2 * x + 2])
+        rd = ["tta", "ttb", "tti", "xl%d" % x]
+        if mul is None:
+            ts(out[:], win, add, None, A.add, None, rd, key)
+        else:
+            ts(out[:], win, mul, add, A.mult, A.add, rd, key)
+
+    def write_list(t, src, dests):
+        moves = []
+        for part in ([d for d in dests if not _near(T, topo, r, d)], [d for d in dests if _near(T, topo, r, d)]):
+            if part:
+                eng = _list_engines(T, topo, r, part[0])
+                ids = [topo.addr(T.cores[d], core) for d in part]
+                moves.append(RemoteDMATransfer(
+                    dst_ids=[DstId(rid=a, pnc=b) for a, b in ids], dma_engine_mask=_mask(eng), remote_sem=T.sem["lst%d_%d" % (t, r)],
+                    srcs=[src], dsts=[T["ll%d" % t][:, K * r:K * r + K] for _ in part]))
+                note("g", "sent", len(eng), [], [])
+        for call in ([moves] if t else [[m] for m in moves]):
+            g.remote_dma_fused(call, local_sem=T.sem.sent)
+
+    dma("s", "dx0", T.xt0[:, 0:4 * H], T.x[:, 0:4 * H], [], ["xt0_0"])
+    dma("a", "dpr", T.pri[:], T.pr[:], [], ["pri"])
+    dma("a", "du", T.ut[:], T.u[:], [], ["ut"])
+    dma("s", "dx1", T.xt0[:, 4 * H:4 * C], T.x[:, 4 * H:4 * C], [], ["xt0_1"])
+    op("g", lambda: g.iota(T.pi[:, 0:1], [[1, 1]], 0, 1), [], ["pi0"])
+    op("g", lambda: g.iota(T.jw[:], [[16, K]], 0, 0, allow_small_or_imprecise_dtypes=True), [], ["jw"])
+    op("g", lambda: g.iota(T.idw[:], [[1, C]], -MID, 0, allow_small_or_imprecise_dtypes=True), [], ["idw"])
+    for i in range(5):
+        op("v", lambda: V.memset(T.ww[:, ROW * i:ROW * i + 16], 0.0), [], ["pad%d" % i])
+    op("v", lambda: V.memset(T.cc[:, 0:32], 0.0), [], ["pad5"])
+    op("v", lambda: V.memset(T.cc[:, 32 + 2 * C:64 + 2 * C], 0.0), [], ["pads"])
+    ts(T.pi[:, 1:2], T.pi[:, 0:1], 15, None, A.bitwise_and, None, ["pi0"], ["pi1"])
+    ts(T.pi[:, 2:3], T.pi[:, 0:1], 1, None, A.bitwise_and, None, ["pi0"], ["pi2"])
+    ts(T.pi[:, 3:4], T.pi[:, 0:1], 4, 1, A.logical_shift_right, A.bitwise_and, ["pi0"], ["pi3"])
+    vcopy(T.pf[:, 0:4], T.pi[:, 0:4], ["pi0", "pi1", "pi2", "pi3"], ["pf"])
+
+    def col(i):
+        return T.pf[:, i:i + 1]
+    op("v", lambda: V.tensor_tensor(col(4), col(2), col(3), A.not_equal), ["pf"], ["pf4"])
+    ts(T.iw[:], T.jw[:], col(1), None, A.add, None, ["jw", "pf"], ["iw"])
+    ts(col(8), col(3), 15.0, 1.0, A.mult, A.add, ["pf"], ["pf8"])
+    ts(col(5), col(4), float(ROW), None, A.mult, None, ["pf4"], ["pf5"])
+    ts(col(6), col(4), float(ROW), 16.0, A.mult, A.add, ["pf4"], ["pf6"])
+    ts(col(9), col(4), float(ROW), -16.0 - 2 * ROW, A.mult, A.add, ["pf4"], ["pf9"])
+    ts(T.ew[:], T.iw[:, 0:2], float(K - 1), None, A.min, None, ["iw"], ["ew"])
+    ts(T.tt[:, 2 * ROW:2 * ROW + K], T.iw[:], -float(MID), None, A.add, None, ["iw"], ["tti"])
+    for i in range(3):
+        vcopy(T.lq[:, K * i:K * i + K], T.iw[:], ["iw"], ["lq%d_%d" % (i, k) for k in range(4)])
+    ts(col(7), col(3), -16.0, col(6), A.mult, A.add, ["pf", "pf6"], ["pf7"])
+    ts(col(10), col(9), col(3), float(2 * ROW), A.mult, A.add, ["pf", "pf9"], ["pf10"])
+    ts(T.xl[:, 4:6], T.ew[:], 16.0, col(5), A.mult, A.add, ["ew", "pf5"], ["xl2"])
+    ts(T.xl[:, 2:4], T.ew[:], 16.0, col(7), A.mult, A.add, ["ew", "pf7"], ["xl1"])
+    ts(T.xl[:, 0:2], T.ew[:], col(8), col(10), A.mult, A.add, ["ew", "pf8", "pf10"], ["xl0"])
+    vcopy(T.prw[:], T.pri[:], ["pri"], ["prw"])
+    acopy(T.d1[:, 1:2 * C:2], T.idw[:], ["idw"], ["d1o"])
+    ts(T.d0[:, 0:2 * C:2], T.idw[:], 0.0, None, A.mult, None, ["idw"], ["d0e"])
+    op("v", lambda: V.tensor_tensor(T.d0[:, 1:2 * C:2], T.idw[:].indirect(T.prw[:]), T.d1[:, 1:2 * C:2], A.subtract), ["idw", "d1o", "prw"], ["d0o"])
+    quant(T.qu, T.su, T.ut, 0, 128, ["ut"], ["qu"])
+    u8, u32 = dt.uint8, dt.uint32
+    dma("s", "dvc", T.qv[:].bitcast(u8), T.vc[:], ["xt0_0", "xt0_1", "ut"], ["qv"])
+    dma("s", "dvs", T.sv[:], T.vs[:], [], ["sv"])
+    dma("s", "dwc", T.qw[:].bitcast(u8), T.wc[:], [], ["qw"])
+    dma("s", "dws", T.sw[:], T.ws[:], [], ["sw"])
+    dma("s", "da", T.at[:], T.a[:], [], ["at"])
+
+    prev, nxt = (r - 1) % N, (r + 1) % N
+    halves = [(0, H), (H, C)]
+    near_prev = _near(T, topo, r, prev)
+    for t in range(ROUNDS):
+        arrives("dat%d" % t, sum(len(e) for e in _data_engines(T, topo, prev)), ["z%d" % t])
+        for s in range(N):
+            if r in _list_dests(s):
+                arrives("lst%d_%d" % (t, s), len(_list_engines(T, topo, s, r)), ["ll%d_%d" % (t, s)])
+
+    def quant_x(t, h):
+        lo, hi = halves[h]
+        quant(T["qx%d" % t], T["sx%d" % t], T["xt%d" % t], lo, hi, ["xt%d_%d" % (t, h)], ["qx%d_%d" % (t, h)])
+
+    def score_mm(t, h):
+        lo, hi = halves[h]
+        for k in range(2):
+            mm(4 + 2 * h + k, T.qu, T.su, 0, T["qx%d" % t], T["sx%d" % t], lo, hi, ["qu", "qx%d_%d" % (t, h)])
+
+    for h in range(2):
+        quant_x(0, h)
+        score_mm(0, h)
+
+    for t in range(ROUNDS):
+        last = t == ROUNDS - 1
+        xt, pl, yt, mx = T["xt%d" % t], T["pl%d" % t], T["yt%d" % t], T["mx%d" % t]
+        qy, sy, qz, sz, qp, sp = [T["%s%d" % (n, t)] for n in ("qy", "sy", "qz", "sz", "qp", "sp")]
+        el, eb, ll = T["el%d" % t], T["eb%d" % t], T["ll%d" % t]
+        xkeys = ["xt0_0", "xt0_1"] if t == 0 else ["xn%d_%d_%d" % (t - 1, h, b) for h in range(2) for b in range(4)]
+
+        def plane(b):
+            acopy(pl[:, C * b:C * b + C], xt[:, b:4 * C:4], xkeys, ["pl%d_%d" % (t, b)])
+
+        for h, (lo, hi) in enumerate(halves):
+            acopy(T.ns[:, lo:hi], bank(5 + 2 * h, H), ["ps%d" % (5 + 2 * h)], ["ns%d" % h], scale=-1.0)
+            vcopy(T.ss[:, lo:hi], bank(4 + 2 * h, H), ["ps%d" % (4 + 2 * h)], ["ss%d" % h])
+        op("v", lambda: V.tensor_tensor(T.d1[:, 0:2 * C:2], T.ss[:].indirect(T.prw[:]), T.ns[:], A.is_gt),
+           ["ss0", "ss1", "ns0", "ns1", "prw"], ["d1e"])
+        for b in range(3):
+            plane(b)
+        op("v", lambda: V.tensor_tensor_scan(T.cc[:, 32:32 + 2 * C], T.d0[:], T.d1[:], 0.0, A.mult, A.add),
+           ["d0e", "d0o", "d1e", "d1o"], ["cc"])
+        turn(T.cc[:, 33:33 + 2 * C:2], T.cc[:, 1:2 * C + 64:2], ["cc"])
+        take(T.e1, 0, ["e1"], 2.0, 2.0 * MID + 1)
+        step(T.cc[:, 32:32 + 2 * C], ["cc"], T.e1, 0, ["e1"], 0)
+        plane(3)
+        turn_row(0)
+        take(T.eq, 1, ["eq"])
+        for i, d0, s0, n in ((0, 96, 64, 32), (0, 64, 32, 32), (1, 64, 0, 64), (2, 96, 0, 32), (2, 32, 0, 32)):
+            vcopy(T.lq[d0:d0 + n, K * i:K * i + K], T.eq[s0:s0 + n, 0:K], ["eq"], ["lq%d_%d" % (i, k) for k in range(d0 // 32, (d0 + n) // 32)])
+            if d0 == 64 and i == 0:
+                step(row(0), wk(0), T.lq, 0, ["lq0_%d" % k for k in range(4)], 1)
+        step(row(1), wk(1), T.lq, K, ["lq1_%d" % k for k in range(4)], 0)
+        step(row(0), wk(0), T.lq, 2 * K, ["lq2_%d" % k for k in range(4)], 1)
+        turn_row(1)
+        elk = ["el%d_%d" % (t, k) for k in range(4)]
+        dests = _list_dests(r)
+        if r < 2 or not dests:
+            take(T.eo, 2, ["eo"])
+        if dests:
+            take(el, 1, elk)
+            if r > 1:
+                take(T.eo, 2, ["eo"])
+            for k in range(3):
+                vcopy(el[32 * k:32 * k + 32, 0:K], el[96:128, 0:K], [elk[3]], [elk[k]])
+            order("g", elk, [])
+            write_list(t, el[:, 0:K], dests)
+
+        rid, pid = topo.addr(T.cores[nxt], core)
+        deng = _data_engines(T, topo, r)
+        for h, (lo, hi) in enumerate(halves):
+            for b in (3, 2, 1, 0):
+                src = pl[:, C * b:C * b + C].indirect(T.eo[:, lo // 16:hi // 16])
+                f = acopy if b >= 2 or (b == 1 and h == 0 and dests) else vcopy
+                f(yt[:, 4 * lo + b:4 * hi:4], src, ["pl%d_%d" % (t, b), "eo"], ["yt%d_%d_%d" % (t, h, b)])
+            quant(qy, sy, yt, lo, hi, ["yt%d_%d_%d" % (t, h, b) for b in range(4)], ["qy%d_%d" % (t, h)])
+            order("g", ["qy%d_%d" % (t, h)], [])
+            g.remote_dma(qz[:, lo:hi].bitcast(u8), qy[:, lo:hi].bitcast(u8), T.sem["dat%d" % t], T.sem.sent, pid, rid, _mask(deng[h]))
+            note("g", "sent", len(deng[h]), [], [])
+        g.remote_dma(sz[:], sy[:], T.sem["dat%d" % t], T.sem.sent, pid, rid, _mask(deng[2]))
+        note("g", "sent", len(deng[2]), [], [])
+        if t == 0:
+            quant(T.qa, T.sa, T.at, 0, 128, ["at"], ["qa"])
+
+        def pick(sq, ssc, lst, l0, lo, hi, reads, key):
+            off = lst[:, l0 + lo // 16:l0 + hi // 16]
+            vcopy(qp[:, lo:hi].bitcast(u32), sq[:].bitcast(u32).indirect(off), reads, ["q" + key])
+            acopy(sp[:, lo:hi], ssc[:].indirect(off), reads, ["s" + key])
+
+        xn = T["xt%d" % (t + 1)]
+        zkey, bkey, pkey = "z%d" % t, "eb%d" % t, "ll%d_%d" % (t, prev)
+        chain = list(range(prev - 1, -1, -1))
+        state = [T.idw[:], ["idw"], 2]
+
+        def steps(n, who):
+            for _ in range(min(n, len(chain))):
+                s = chain.pop(0)
+                win, wkeys, i = state
+                if s == r:
+                    step(win, wkeys, el, 0, elk, i, who)
+                else:
+                    step(win, wkeys, ll, K * s, ["ll%d_%d" % (t, s)], i, who)
+                state[0], state[1], state[2] = row(i), wk(i), 5 - i
+
+        def wrap_b():
+            turn_row(5 - state[2])
+            take(eb, 1, [bkey])
+
+        ykeys = ["qy%d_0" % t, "qy%d_1" % t]
+        if t and r > 1 and near_prev:
+            steps(1, "s")
+        if r:
+            pick(qy, sy, ll, K * prev, 0, C, ykeys + [pkey], "p%d" % t)
+            vq, vsc, vkeys = qp, sp, ["qp%d" % t, "sp%d" % t]
+        else:
+            vq, vsc, vkeys = qy, sy, ykeys
+        for b in range(4):
+            mm(b, T.qv, T.sv, 128 * b, vq, vsc, 0, C, ["qv", "sv"] + vkeys)
+        share = r < 2 or (near_prev and not t)
+        for b in range(4):
+            (vcopy if share and b % 2 else acopy)(T.pvs[:, C * b:C * b + C], bank(b, C), ["ps%d" % b], ["pvs%d" % b])
+
+        def wbank(h, b):
+            return 4 * (1 - h) + b
+
+        def by_w(h, q, s, keys):
+            lo, hi = halves[h]
+            for b in range(4):
+                mm(wbank(h, b), T.qw, T.sw, 128 * b, q, s, lo, hi, ["qw", "sw"] + keys)
+
+        def larger(h, b):
+            lo, hi = halves[h]
+            k = wbank(h, b)
+            op("v", lambda: V.tensor_tensor(mx[:, C * b + lo:C * b + hi], bank(k, H), T.pvs[:, C * b + lo:C * b + hi], A.max),
+               ["ps%d" % k, "pvs%d" % b], ["mx%d_%d_%d" % (t, h, b)])
+
+        def place(who, h, b):
+            lo, hi = halves[h]
+            rd = ["mx%d_%d_%d" % (t, k, b) for k in range(2)] + [bkey]
+            src = mx[:, C * b:C * b + C].indirect(eb[:, lo // 16:hi // 16])
+            key = ["xn%d_%d_%d" % (t, h, b)]
+            if who == "a":
+                acopy(xn[:, 4 * lo + b:4 * hi:4], src, rd, key, scale=SCALE)
+            else:
+                ts(xn[:, 4 * lo + b:4 * hi:4], src, SCALE, None, A.mult, None, rd, key)
+
+        def after(h):
+            order("v", ["xn%d_%d_%d" % (t, h, b) for b in range(4)], [])
+            quant_x(t + 1, h)
+            lo, hi = halves[h]
+            if not last:
+                score_mm(t + 1, h)
+            else:
+                mm(4 + h, T.qa, T.sa, 0, T["qx%d" % ROUNDS], T["sx%d" % ROUNDS], lo, hi, ["qa", "qx%d_%d" % (ROUNDS, h)])
+                dma("s", "outs", T.oc[:, 4 * lo:4 * hi], T["qx%d" % ROUNDS][:, lo:hi].bitcast(u8), ["qx%d_%d" % (ROUNDS, h)], [])
+
+        def store_lists(src, reads):
+            acopy(T.ols[:], src, reads, ["ols"], bias=float(MID))
+            dma("s", "outs", T.ol[:], T.ols[0:128:16, :], ["ols"], [])
+
+        if r < 2:
+            if r == 0:
+                if last:
+                    store_lists(row(1), wk(1))
+                steps(N, "s")
+                wrap_b()
+                for h, (lo, hi) in enumerate(halves):
+                    pick(qz, sz, eb, 0, lo, hi, [zkey, bkey], "p%d_%d" % (t, h))
+                    by_w(h, qp, sp, ["qp%d_%d" % (t, h), "sp%d_%d" % (t, h)])
+            else:
+                if last:
+                    store_lists(row(1).indirect(ll[:, K * prev:K * prev + K]), wk(1) + [pkey])
+                for h in range(2):
+                    by_w(h, qz, sz, [zkey])
+            for h, (lo, hi) in enumerate(halves):
+                for b in range(4):
+                    larger(h, b)
+                    acopy(xn[:, 4 * lo + b:4 * hi:4], mx[:, C * b + lo:C * b + hi], ["mx%d_%d_%d" % (t, h, b)],
+                          ["xn%d_%d_%d" % (t, h, b)], scale=SCALE)
+                    if (h, b) == (1, 1):
+                        after(0)
+            after(1)
+        else:
+            if near_prev:
+                for h in range(2):
+                    by_w(h, qz, sz, [zkey])
+                if t:
+                    steps(2, "v")
+                steps(2, "a")
+                for h in range(2):
+                    for b in range(4):
+                        larger(h, b)
+            else:
+                steps(3, "v")
+            steps(N, "s")
+            if last:
+                acopy(T.ow[:], row(1).indirect(ll[:, K * prev:K * prev + K]), wk(1) + [pkey], ["ow"])
+            wrap_b()
+            if near_prev:
+                for h in range(2):
+                    for b in range(4):
+                        place("a" if b % 2 else "v", h, b)
+                    after(h)
+            else:
+                for h in range(2):
+                    by_w(h, qz, sz, [zkey])
+                for b in range(4):
+                    larger(0, b)
+                    larger(1, b)
+                    if b < 3:
+                        place("a", 0, b)
+                    if b < 2:
+                        place("a", 1, b)
+                place("a", 1, 2)
+                for h in range(2):
+                    place("v", h, 3)
+                    after(h)
+            if last:
+                store_lists(T.ow[:].indirect(eb[:, 0:K]), ["ow", bkey])
+
+    fk = ["qx%d_0" % ROUNDS, "qx%d_1" % ROUNDS]
+    for k in range(4):
+        dma("s", "outs", T.osc[4 * k:4 * k + 4, :], T["sx%d" % ROUNDS][32 * k:32 * k + 4, :], fk, [])
+    acopy(T.ys[:, 0:H], bank(4, H), ["ps4"], ["ys0"])
+    vcopy(T.ys[:, H:C], bank(5, H), ["ps5"], ["ys1"])
+    for h, (lo, hi) in enumerate(halves):
+        dma("a", "outa", T.y[:, lo:hi], T.ys[:, lo:hi], ["ys%d" % h], [])
+    for sem, n in count.items():
+        if waited.get(sem, 0) < n:
+            g.wait_ge(T.sem[sem], n)

@@ -6,6 +6,7 @@ H = C // 2
 K = C // 16
 MID = C // 2
 ROW = C + 16
+CUT = 2 * C // 3
 SCALE = 0.03125
 CODES, PLANE = "float8_e4m3fn_x4", "uint8"
 
@@ -17,9 +18,9 @@ SCRATCH = {
     "qv": ("sbuf", [128, 512], CODES), "sv": ("sbuf", [128, 512], PLANE),
     "qw": ("sbuf", [128, 512], CODES), "sw": ("sbuf", [128, 512], PLANE),
     "pri": ("sbuf", [128, K], "int32"), "prw": ("sbuf", [128, K], "uint16"),
-    "pi": ("sbuf", [128, 4], "int32"), "pf": ("sbuf", [128, 12], "float32"),
-    "jw": ("sbuf", [128, K], "float32"), "iw": ("sbuf", [128, K], "float32"), "ew": ("sbuf", [128, 2], "float32"),
-    "xl": ("sbuf", [128, 6], "uint16"),
+    "pi": ("sbuf", [128, 4], "int32"), "pf": ("sbuf", [128, 16], "float32"),
+    "jw": ("sbuf", [128, 3 * K], "float32"), "iw": ("sbuf", [128, K], "float32"), "ew": ("sbuf", [128, 2], "float32"),
+    "xl": ("sbuf", [128, 10], "uint16"),
     "idw": ("sbuf", [128, C], "bfloat16"),
     "d0": ("sbuf", [128, 2 * C], "float16"), "d1": ("sbuf", [128, 2 * C], "bfloat16"),
     "cc": ("sbuf", [128, 2 * C + 64], "bfloat16"),
@@ -42,8 +43,8 @@ for _t in range(ROUNDS):
     for _n in ("y", "z", "p"):
         SCRATCH["q%s%d" % (_n, _t)] = ("sbuf", [128, C], CODES)
         SCRATCH["s%s%d" % (_n, _t)] = ("sbuf", [128, C], PLANE)
-    SCRATCH["el%d" % _t] = ("sbuf", [128, 32], "uint16")
-    SCRATCH["eb%d" % _t] = ("sbuf", [128, 32], "uint16")
+    for _n in ("el", "es", "eb"):
+        SCRATCH["%s%d" % (_n, _t)] = ("sbuf", [128, 32], "uint16")
     SCRATCH["ll%d" % _t] = ("sbuf", [128, (N - 1) * K], "uint16")
 
 SEMAPHORES = (["cv", "ca", "cp", "cg", "sent", "dx0", "dx1", "du", "dpr", "dvc", "dvs", "dwc", "dws", "da", "outs", "outa"]
@@ -79,7 +80,7 @@ def _data_engines(T, topo, r):
     far, near = _lanes(T, topo, r)
     if _near(T, topo, r, (r + 1) % N):
         return [near, far + near, far + near]
-    return [far, far, far]
+    return [far, far] if _list_dests(r) else [far, far, far]
 
 
 def _list_engines(T, topo, s, d):
@@ -219,9 +220,9 @@ def rank_program(g, core, T, topo):
     dma("a", "du", T.ut[:], T.u[:], [], ["ut"])
     dma("s", "dx1", T.xt0[:, 4 * H:4 * C], T.x[:, 4 * H:4 * C], [], ["xt0_1"])
     op("g", lambda: g.iota(T.pi[:, 0:1], [[1, 1]], 0, 1), [], ["pi0"])
-    op("g", lambda: g.iota(T.jw[:], [[16, K]], 0, 0, allow_small_or_imprecise_dtypes=True), [], ["jw"])
+    op("g", lambda: g.iota(T.jw[:], [[0, 3], [16, K]], 0, 0, allow_small_or_imprecise_dtypes=True), [], ["jw"])
     op("g", lambda: g.iota(T.idw[:], [[1, C]], -MID, 0, allow_small_or_imprecise_dtypes=True), [], ["idw"])
-    for i in range(5):
+    for i in range(3):
         op("v", lambda: V.memset(T.ww[:, ROW * i:ROW * i + 16], 0.0), [], ["pad%d" % i])
     op("v", lambda: V.memset(T.cc[:, 0:32], 0.0), [], ["pad5"])
     op("v", lambda: V.memset(T.cc[:, 32 + 2 * C:64 + 2 * C], 0.0), [], ["pads"])
@@ -233,18 +234,23 @@ def rank_program(g, core, T, topo):
     def col(i):
         return T.pf[:, i:i + 1]
     op("v", lambda: V.tensor_tensor(col(4), col(2), col(3), A.not_equal), ["pf"], ["pf4"])
-    ts(T.iw[:], T.jw[:], col(1), None, A.add, None, ["jw", "pf"], ["iw"])
+    ts(T.iw[:], T.jw[:, 0:K], col(1), None, A.add, None, ["jw", "pf"], ["iw"])
     ts(col(8), col(3), 15.0, 1.0, A.mult, A.add, ["pf"], ["pf8"])
+    if r == 0:
+        ts(col(11), col(3), -32.0, float(ROW), A.mult, A.add, ["pf"], ["pf11"])
     ts(col(5), col(4), float(ROW), None, A.mult, None, ["pf4"], ["pf5"])
     ts(col(6), col(4), float(ROW), 16.0, A.mult, A.add, ["pf4"], ["pf6"])
     ts(col(9), col(4), float(ROW), -16.0 - 2 * ROW, A.mult, A.add, ["pf4"], ["pf9"])
+    if r == 0:
+        ts(col(12), col(11), col(2), 16.0, A.mult, A.add, ["pf", "pf11"], ["pf12"])
     ts(T.ew[:], T.iw[:, 0:2], float(K - 1), None, A.min, None, ["iw"], ["ew"])
     ts(T.tt[:, 2 * ROW:2 * ROW + K], T.iw[:], -float(MID), None, A.add, None, ["iw"], ["tti"])
-    for i in range(3):
-        vcopy(T.lq[:, K * i:K * i + K], T.iw[:], ["iw"], ["lq%d_%d" % (i, k) for k in range(4)])
+    ts(T.lq[:], T.jw[:], col(1), None, A.add, None, ["jw", "pf"], ["lq%d_%d" % (i, k) for i in range(3) for k in range(4)])
     ts(col(7), col(3), -16.0, col(6), A.mult, A.add, ["pf", "pf6"], ["pf7"])
     ts(col(10), col(9), col(3), float(2 * ROW), A.mult, A.add, ["pf", "pf9"], ["pf10"])
     ts(T.xl[:, 4:6], T.ew[:], 16.0, col(5), A.mult, A.add, ["ew", "pf5"], ["xl2"])
+    if r == 0:
+        ts(T.xl[:, 6:8], T.ew[:], 16.0, col(12), A.mult, A.add, ["ew", "pf12"], ["xl3"])
     ts(T.xl[:, 2:4], T.ew[:], 16.0, col(7), A.mult, A.add, ["ew", "pf7"], ["xl1"])
     ts(T.xl[:, 0:2], T.ew[:], col(8), col(10), A.mult, A.add, ["ew", "pf8", "pf10"], ["xl0"])
     vcopy(T.prw[:], T.pri[:], ["pri"], ["prw"])
@@ -261,6 +267,7 @@ def rank_program(g, core, T, topo):
 
     prev, nxt = (r - 1) % N, (r + 1) % N
     halves = [(0, H), (H, C)]
+    parts = [(0, CUT), (CUT, C)]
     near_prev = _near(T, topo, r, prev)
     for t in range(ROUNDS):
         arrives("dat%d" % t, sum(len(e) for e in _data_engines(T, topo, prev)), ["z%d" % t])
@@ -269,11 +276,11 @@ def rank_program(g, core, T, topo):
                 arrives("lst%d_%d" % (t, s), len(_list_engines(T, topo, s, r)), ["ll%d_%d" % (t, s)])
 
     def quant_x(t, h):
-        lo, hi = halves[h]
+        lo, hi = (parts if t else halves)[h]
         quant(T["qx%d" % t], T["sx%d" % t], T["xt%d" % t], lo, hi, ["xt%d_%d" % (t, h)], ["qx%d_%d" % (t, h)])
 
     def score_mm(t, h):
-        lo, hi = halves[h]
+        lo, hi = (parts if t else halves)[h]
         for k in range(2):
             mm(4 + 2 * h + k, T.qu, T.su, 0, T["qx%d" % t], T["sx%d" % t], lo, hi, ["qu", "qx%d_%d" % (t, h)])
 
@@ -285,15 +292,15 @@ def rank_program(g, core, T, topo):
         last = t == ROUNDS - 1
         xt, pl, yt, mx = T["xt%d" % t], T["pl%d" % t], T["yt%d" % t], T["mx%d" % t]
         qy, sy, qz, sz, qp, sp = [T["%s%d" % (n, t)] for n in ("qy", "sy", "qz", "sz", "qp", "sp")]
-        el, eb, ll = T["el%d" % t], T["eb%d" % t], T["ll%d" % t]
+        el, es, eb, ll = T["el%d" % t], T["es%d" % t], T["eb%d" % t], T["ll%d" % t]
         xkeys = ["xt0_0", "xt0_1"] if t == 0 else ["xn%d_%d_%d" % (t - 1, h, b) for h in range(2) for b in range(4)]
 
         def plane(b):
             acopy(pl[:, C * b:C * b + C], xt[:, b:4 * C:4], xkeys, ["pl%d_%d" % (t, b)])
 
-        for h, (lo, hi) in enumerate(halves):
-            acopy(T.ns[:, lo:hi], bank(5 + 2 * h, H), ["ps%d" % (5 + 2 * h)], ["ns%d" % h], scale=-1.0)
-            vcopy(T.ss[:, lo:hi], bank(4 + 2 * h, H), ["ps%d" % (4 + 2 * h)], ["ss%d" % h])
+        for h, (lo, hi) in enumerate(parts if t else halves):
+            acopy(T.ns[:, lo:hi], bank(5 + 2 * h, hi - lo), ["ps%d" % (5 + 2 * h)], ["ns%d" % h], scale=-1.0)
+            vcopy(T.ss[:, lo:hi], bank(4 + 2 * h, hi - lo), ["ps%d" % (4 + 2 * h)], ["ss%d" % h])
         op("v", lambda: V.tensor_tensor(T.d1[:, 0:2 * C:2], T.ss[:].indirect(T.prw[:]), T.ns[:], A.is_gt),
            ["ss0", "ss1", "ns0", "ns1", "prw"], ["d1e"])
         for b in range(3):
@@ -314,17 +321,22 @@ def rank_program(g, core, T, topo):
         step(row(0), wk(0), T.lq, 2 * K, ["lq2_%d" % k for k in range(4)], 1)
         turn_row(1)
         elk = ["el%d_%d" % (t, k) for k in range(4)]
+        esk = ["es%d_%d" % (t, k) for k in range(4)]
         dests = _list_dests(r)
         if r < 2 or not dests:
             take(T.eo, 2, ["eo"])
-        if dests:
-            take(el, 1, elk)
-            if r > 1:
-                take(T.eo, 2, ["eo"])
+
+        def spread(buf, x, keys, between=None):
+            take(buf, x, keys)
+            if between:
+                between()
             for k in range(3):
-                vcopy(el[32 * k:32 * k + 32, 0:K], el[96:128, 0:K], [elk[3]], [elk[k]])
-            order("g", elk, [])
-            write_list(t, el[:, 0:K], dests)
+                vcopy(buf[32 * k:32 * k + 32, 0:K], buf[96:128, 0:K], [keys[3]], [keys[k]])
+            order("g", keys, [])
+
+        if dests:
+            spread(el, 1, elk, (lambda: take(T.eo, 2, ["eo"])) if r > 1 else None)
+            write_list(t, el[:, 0:K], dests if r else dests[:1])
 
         rid, pid = topo.addr(T.cores[nxt], core)
         deng = _data_engines(T, topo, r)
@@ -334,13 +346,21 @@ def rank_program(g, core, T, topo):
                 f = acopy if b >= 2 or (b == 1 and h == 0 and dests) else vcopy
                 f(yt[:, 4 * lo + b:4 * hi:4], src, ["pl%d_%d" % (t, b), "eo"], ["yt%d_%d_%d" % (t, h, b)])
             quant(qy, sy, yt, lo, hi, ["yt%d_%d_%d" % (t, h, b) for b in range(4)], ["qy%d_%d" % (t, h)])
-            order("g", ["qy%d_%d" % (t, h)], [])
-            g.remote_dma(qz[:, lo:hi].bitcast(u8), qy[:, lo:hi].bitcast(u8), T.sem["dat%d" % t], T.sem.sent, pid, rid, _mask(deng[h]))
-            note("g", "sent", len(deng[h]), [], [])
-        g.remote_dma(sz[:], sy[:], T.sem["dat%d" % t], T.sem.sent, pid, rid, _mask(deng[2]))
-        note("g", "sent", len(deng[2]), [], [])
+            if len(deng) == 3 or h:
+                a, e = (lo, deng[h]) if len(deng) == 3 else (0, deng[0])
+                order("g", ["qy%d_%d" % (t, h)], [])
+                g.remote_dma(qz[:, a:hi].bitcast(u8), qy[:, a:hi].bitcast(u8), T.sem["dat%d" % t], T.sem.sent, pid, rid, _mask(e))
+                note("g", "sent", len(e), [], [])
+            if r == 0 and h == 0:
+                spread(es, 3, esk)
+                write_list(t, es[:, 0:K], dests[1:])
+        g.remote_dma(sz[:], sy[:], T.sem["dat%d" % t], T.sem.sent, pid, rid, _mask(deng[-1]))
+        note("g", "sent", len(deng[-1]), [], [])
         if t == 0:
+            ts(col(13), col(2), -32.0, 16.0, A.mult, A.add, ["pf"], ["pf13"])
             quant(T.qa, T.sa, T.at, 0, 128, ["at"], ["qa"])
+            ts(col(14), col(13), col(3), None, A.mult, None, ["pf", "pf13"], ["pf14"])
+            ts(T.xl[:, 8:10], T.ew[:], 16.0, col(14), A.mult, A.add, ["ew", "pf14"], ["xl4"])
 
         def pick(sq, ssc, lst, l0, lo, hi, reads, key):
             off = lst[:, l0 + lo // 16:l0 + hi // 16]
@@ -357,45 +377,50 @@ def rank_program(g, core, T, topo):
                 s = chain.pop(0)
                 win, wkeys, i = state
                 if s == r:
-                    step(win, wkeys, el, 0, elk, i, who)
+                    step(win, wkeys, es, 0, esk, i, who)
                 else:
                     step(win, wkeys, ll, K * s, ["ll%d_%d" % (t, s)], i, who)
                 state[0], state[1], state[2] = row(i), wk(i), 5 - i
 
         def wrap_b():
-            turn_row(5 - state[2])
-            take(eb, 1, [bkey])
+            i = 5 - state[2]
+            op("v", lambda: V.transpose(T.tt[:, 0:C], row(i)), wk(i), ["tta"])
+            take(eb, 4, [bkey])
 
         ykeys = ["qy%d_0" % t, "qy%d_1" % t]
         if t and r > 1 and near_prev:
             steps(1, "s")
         if r:
             pick(qy, sy, ll, K * prev, 0, C, ykeys + [pkey], "p%d" % t)
-            vq, vsc, vkeys = qp, sp, ["qp%d" % t, "sp%d" % t]
+            for b in range(4):
+                mm(b, T.qv, T.sv, 128 * b, qp, sp, 0, C, ["qv", "sv", "qp%d" % t, "sp%d" % t])
+            share = near_prev or t > 0
+            for b in range(4):
+                (vcopy if share and b % 2 else acopy)(T.pvs[:, C * b:C * b + C], bank(b, C), ["ps%d" % b], ["pvs%d" % b, "pvt%d" % b])
         else:
-            vq, vsc, vkeys = qy, sy, ykeys
-        for b in range(4):
-            mm(b, T.qv, T.sv, 128 * b, vq, vsc, 0, C, ["qv", "sv"] + vkeys)
-        share = r < 2 or (near_prev and not t)
-        for b in range(4):
-            (vcopy if share and b % 2 else acopy)(T.pvs[:, C * b:C * b + C], bank(b, C), ["ps%d" % b], ["pvs%d" % b])
+            for h, (lo, hi) in enumerate(halves):
+                for b in range(4):
+                    mm(4 * h + b, T.qv, T.sv, 128 * b, qy, sy, lo, hi, ["qv", "sv", ykeys[h]])
+                for b in range(4):
+                    (vcopy if h and b % 2 else acopy)(T.pvs[:, C * b + lo:C * b + hi], bank(4 * h + b, H), ["ps%d" % (4 * h + b)],
+                                                      ["pv%s%d" % ("st"[h], b)])
 
         def wbank(h, b):
             return 4 * (1 - h) + b
 
         def by_w(h, q, s, keys):
-            lo, hi = halves[h]
+            lo, hi = parts[h]
             for b in range(4):
                 mm(wbank(h, b), T.qw, T.sw, 128 * b, q, s, lo, hi, ["qw", "sw"] + keys)
 
         def larger(h, b):
-            lo, hi = halves[h]
+            lo, hi = parts[h]
             k = wbank(h, b)
-            op("v", lambda: V.tensor_tensor(mx[:, C * b + lo:C * b + hi], bank(k, H), T.pvs[:, C * b + lo:C * b + hi], A.max),
-               ["ps%d" % k, "pvs%d" % b], ["mx%d_%d_%d" % (t, h, b)])
+            op("v", lambda: V.tensor_tensor(mx[:, C * b + lo:C * b + hi], bank(k, hi - lo), T.pvs[:, C * b + lo:C * b + hi], A.max),
+               ["ps%d" % k, "pvs%d" % b, "pvt%d" % b], ["mx%d_%d_%d" % (t, h, b)])
 
         def place(who, h, b):
-            lo, hi = halves[h]
+            lo, hi = parts[h]
             rd = ["mx%d_%d_%d" % (t, k, b) for k in range(2)] + [bkey]
             src = mx[:, C * b:C * b + C].indirect(eb[:, lo // 16:hi // 16])
             key = ["xn%d_%d_%d" % (t, h, b)]
@@ -407,7 +432,7 @@ def rank_program(g, core, T, topo):
         def after(h):
             order("v", ["xn%d_%d_%d" % (t, h, b) for b in range(4)], [])
             quant_x(t + 1, h)
-            lo, hi = halves[h]
+            lo, hi = parts[h]
             if not last:
                 score_mm(t + 1, h)
             else:
@@ -416,15 +441,16 @@ def rank_program(g, core, T, topo):
 
         def store_lists(src, reads):
             acopy(T.ols[:], src, reads, ["ols"], bias=float(MID))
-            dma("s", "outs", T.ol[:], T.ols[0:128:16, :], ["ols"], [])
+            if r < 2:
+                dma("s", "outs", T.ol[:], T.ols[0:128:16, :], ["ols"], [])
 
         if r < 2:
             if r == 0:
+                steps(N, "s")
                 if last:
                     store_lists(row(1), wk(1))
-                steps(N, "s")
                 wrap_b()
-                for h, (lo, hi) in enumerate(halves):
+                for h, (lo, hi) in enumerate(parts):
                     pick(qz, sz, eb, 0, lo, hi, [zkey, bkey], "p%d_%d" % (t, h))
                     by_w(h, qp, sp, ["qp%d_%d" % (t, h), "sp%d_%d" % (t, h)])
             else:
@@ -432,25 +458,24 @@ def rank_program(g, core, T, topo):
                     store_lists(row(1).indirect(ll[:, K * prev:K * prev + K]), wk(1) + [pkey])
                 for h in range(2):
                     by_w(h, qz, sz, [zkey])
-            for h, (lo, hi) in enumerate(halves):
+            for h, (lo, hi) in enumerate(parts):
                 for b in range(4):
                     larger(h, b)
                     acopy(xn[:, 4 * lo + b:4 * hi:4], mx[:, C * b + lo:C * b + hi], ["mx%d_%d_%d" % (t, h, b)],
                           ["xn%d_%d_%d" % (t, h, b)], scale=SCALE)
-                    if (h, b) == (1, 1):
-                        after(0)
+            after(0)
             after(1)
         else:
             if near_prev:
+                if t:
+                    steps(len(chain) - 2, "s")
                 for h in range(2):
                     by_w(h, qz, sz, [zkey])
-                if t:
-                    steps(2, "v")
                 steps(2, "a")
                 for h in range(2):
                     for b in range(4):
                         larger(h, b)
-            else:
+            elif not t:
                 steps(3, "v")
             steps(N, "s")
             if last:
@@ -479,12 +504,20 @@ def rank_program(g, core, T, topo):
                 store_lists(T.ow[:].indirect(eb[:, 0:K]), ["ow", bkey])
 
     fk = ["qx%d_0" % ROUNDS, "qx%d_1" % ROUNDS]
-    for k in range(4):
-        dma("s", "outs", T.osc[4 * k:4 * k + 4, :], T["sx%d" % ROUNDS][32 * k:32 * k + 4, :], fk, [])
-    acopy(T.ys[:, 0:H], bank(4, H), ["ps4"], ["ys0"])
-    vcopy(T.ys[:, H:C], bank(5, H), ["ps5"], ["ys1"])
-    for h, (lo, hi) in enumerate(halves):
-        dma("a", "outa", T.y[:, lo:hi], T.ys[:, lo:hi], ["ys%d" % h], [])
+
+    def scales(q, sem, k):
+        dma(q, sem, T.osc[4 * k:4 * k + 4, :], T["sx%d" % ROUNDS][32 * k:32 * k + 4, :], fk, [])
+
+    scales("s", "outs", 0)
+    scales("s", "outs", 1)
+    if r >= 2:
+        dma("s", "outs", T.ol[:], T.ols[0:128:16, :], ["ols"], [])
+    acopy(T.ys[:, 0:CUT], bank(4, CUT), ["ps4"], ["ys0"])
+    vcopy(T.ys[:, CUT:C], bank(5, C - CUT), ["ps5"], ["ys1"])
+    dma("a", "outa", T.y[:, 0:CUT], T.ys[:, 0:CUT], ["ys0"], [])
+    scales("a", "outa", 2)
+    scales("a", "outa", 3)
+    dma("a", "outa", T.y[:, CUT:C], T.ys[:, CUT:C], ["ys1"], [])
     for sem, n in count.items():
         if waited.get(sem, 0) < n:
             g.wait_ge(T.sem[sem], n)

from concourse.bass import DstId, RemoteDMATransfer
from concourse.mybir import dt, AluOpType, ActivationFunctionType

N, C, ROUNDS = 8, 384, 2
H = C // 2
K = C // 16
MID = C // 2
ROW = C + 16
CUT = 2 * C // 3
SCALE = 0.03125
CODES, PLANE = "float8_e4m3fn_x4", "uint8"

SCRATCH = {
    "xt0": ("sbuf", [128, 4 * C], "bfloat16"), "xt1": ("sbuf", [128, 4 * C], "bfloat16"), "xt2": ("sbuf", [128, 4 * C], "bfloat16"),
    "ut": ("sbuf", [128, 512], "bfloat16"), "at": ("sbuf", [128, 512], "bfloat16"),
    "qu": ("sbuf", [128, 128], CODES), "su": ("sbuf", [128, 128], PLANE),
    "qa": ("sbuf", [128, 128], CODES), "sa": ("sbuf", [128, 128], PLANE),
    "qv": ("sbuf", [128, 512], CODES), "sv": ("sbuf", [128, 512], PLANE),
    "qw": ("sbuf", [128, 512], CODES), "sw": ("sbuf", [128, 512], PLANE),
    "pri": ("sbuf", [128, K], "int32"), "prw": ("sbuf", [128, K], "uint16"),
    "pi": ("sbuf", [128, 4], "int32"), "pf": ("sbuf", [128, 16], "float32"),
    "jw": ("sbuf", [128, 3 * K], "float32"), "iw": ("sbuf", [128, K], "float32"), "ew": ("sbuf", [128, 2], "float32"),
    "xl": ("sbuf", [128, 10], "uint16"),
    "idw": ("sbuf", [128, C], "bfloat16"),
    "d0": ("sbuf", [128, 2 * C], "float16"), "d1": ("sbuf", [128, 2 * C], "bfloat16"),
    "cc": ("sbuf", [128, 2 * C + 64], "bfloat16"),
    "ww": ("sbuf", [128, 4 * ROW + 16], "bfloat16"), "ow": ("sbuf", [128, C], "bfloat16"),
    "tt": ("sbuf", [128, 2 * ROW + K], "bfloat16"),
    "ss": ("sbuf", [128, C], "float32"), "ns": ("sbuf", [128, C], "float32"),
    "e1": ("sbuf", [128, 32], "uint16"), "eq": ("sbuf", [128, 32], "uint16"), "eo": ("sbuf", [128, 32], "uint16"),
    "lq": ("sbuf", [128, 3 * K], "uint16"),
    "pvs": ("sbuf", [128, 4 * C], "float32"),
    "ys": ("sbuf", [128, C], "float32"), "ols": ("sbuf", [128, C], "float32"),
    "ps": ("psum", [128, 8 * 512], "float32"),
}
for _t in range(ROUNDS + 1):
    SCRATCH["qx%d" % _t] = ("sbuf", [128, C], CODES)
    SCRATCH["sx%d" % _t] = ("sbuf", [128, C], PLANE)
for _t in range(ROUNDS):
    SCRATCH["pl%d" % _t] = ("sbuf", [128, 4 * C], "bfloat16")
    SCRATCH["yt%d" % _t] = ("sbuf", [128, 4 * C], "bfloat16")
    SCRATCH["mx%d" % _t] = ("sbuf", [128, 4 * C], "float32")
    for _n in ("y", "z", "p"):
        SCRATCH["q%s%d" % (_n, _t)] = ("sbuf", [128, C], CODES)
        SCRATCH["s%s%d" % (_n, _t)] = ("sbuf", [128, C], PLANE)
    for _n in ("el", "es", "eb"):
        SCRATCH["%s%d" % (_n, _t)] = ("sbuf", [128, 32], "uint16")
    SCRATCH["ll%d" % _t] = ("sbuf", [128, (N - 1) * K], "uint16")

SEMAPHORES = (["cv", "ca", "cp", "cg", "sent", "dx0", "dx1", "du", "dpr", "dvc", "dvs", "dwc", "dws", "da", "outs", "outa"]
              + ["dat%d" % t for t in range(ROUNDS)] + ["lst%d_%d" % (t, s) for t in range(ROUNDS) for s in range(N - 1)])


def _mask(engines):
    m = 0
    for e in engines:
        m |= 1 << e
    return m


def _near(T, topo, a, b):
    return T.cores[b] in topo.cores_of(T.cores[a])


def _lanes(T, topo, r):
    me = T.cores[r]
    own = topo.cores_of(me)
    far = topo.engines(me, [c for c in T.cores if c not in own][0])
    near = [e for e in topo.engines(me, [c for c in own if c != me][0]) if e not in far]
    return far, near


def _list_dests(s):
    if s == N - 1:
        return []
    return ([0] if s else []) + list(range(s + 1, N))


def _data_engines(T, topo, r):
    far, near = _lanes(T, topo, r)
    if _near(T, topo, r, (r + 1) % N):
        return [near, far + near, far + near]
    return [far, far] if _list_dests(r) else [far, far, far]


def _list_engines(T, topo, s, d):
    far, near = _lanes(T, topo, s)
    return near if _near(T, topo, s, d) else far


def rank_program(g, core, T, topo):
    r = T.rank_of(core)
    if r is None:
        return
    A, F = AluOpType, ActivationFunctionType
    V, S, P = g.vector, g.scalar, g.tensor
    queue = {"v": V, "a": S, "p": P, "g": g, "s": g.sync}
    known = {q: {} for q in queue}
    count, waited = {}, {}
    writer, readers = {}, {}

    def wait(q, ev):
        sem, n, clock, _ = ev
        if known[q].get(sem, 0) < n:
            queue[q].wait_ge(T.sem[sem], n)
            waited[sem] = max(waited.get(sem, 0), n)
        for k, v in clock.items():
            if known[q].get(k, 0) < v:
                known[q][k] = v

    def order(q, reads, writes):
        deps = [writer[k] for k in reads + writes if k in writer]
        for k in writes:
            deps += readers.get(k, [])
        for k in reads:
            if k.startswith("ps"):
                deps += [e for e in readers.get(k, []) if e[3] != q]
        top = {}
        for e in deps:
            if e[0] not in top or top[e[0]][1] < e[1]:
                top[e[0]] = e
        for e in top.values():
            wait(q, e)

    def note(q, sem, inc, reads, writes):
        count[sem] = count.get(sem, 0) + inc
        clock = dict(known[q])
        clock[sem] = count[sem]
        ev = (sem, count[sem], clock, q)
        for k in reads:
            readers.setdefault(k, []).append(ev)
        for k in writes:
            writer[k] = ev
            readers[k] = []

    def op(q, fn, reads, writes):
        order(q, reads, writes)
        fn().then_inc(T.sem["c" + q], 1)
        note(q, "c" + q, 1, reads, writes)

    def dma(q, sem, out, in_, reads, writes):
        order(q, reads, writes)
        queue[q].dma_start(out, in_).then_inc(T.sem[sem], 16)
        note(q, sem, 16, reads, writes)

    def arrives(sem, n, keys):
        count[sem] = n
        for k in keys:
            writer[k] = (sem, n, {sem: n}, "far")

    def bank(b, n):
        return T.ps[:, 512 * b:512 * b + n]

    def ts(out, in0, s1, s2, o0, o1, reads, writes):
        if o1 is None:
            op("v", lambda: V.tensor_scalar(out, in0, s1, None, o0), reads, writes)
        else:
            op("v", lambda: V.tensor_scalar(out, in0, s1, s2, o0, o1), reads, writes)

    def vcopy(out, in_, reads, writes):
        op("v", lambda: V.tensor_copy(out, in_), reads, writes)

    def acopy(out, in_, reads, writes, **kw):
        f = F.Identity if "bias" in kw else F.Copy
        op("a", lambda: S.activation(out, in_, f, **kw), reads, writes)

    def quant(q, s, tile, lo, hi, reads, writes):
        op("v", lambda: V.quantize_mx(q[:, lo:hi], s[:, lo:hi], tile[:, 4 * lo:4 * hi]), reads, writes)

    def mm(b, lq, ls, l0, rq, rs, lo, hi, reads):
        op("p", lambda: P.matmul_mx(bank(b, hi - lo), lq[:, l0:l0 + 128], ls[:, l0:l0 + 128], rq[:, lo:hi], rs[:, lo:hi], True, True),
           reads, ["ps%d" % b])

    def row(i):
        return T.ww[:, ROW * i + 16:ROW * i + 16 + C]

    def rowpart(i, lo, hi):
        return T.ww[:, ROW * i + 16 + lo:ROW * i + 16 + hi]

    def wk(i):
        return ["w%d_0" % i, "w%d_1" % i]

    def step(win, wkeys, lst, l0, lkeys, i, who="s"):
        if who == "s":
            vcopy(rowpart(i, 0, H), win.indirect(lst[:, l0:l0 + K // 2]), wkeys + lkeys, ["w%d_0" % i])
            acopy(rowpart(i, H, C), win.indirect(lst[:, l0 + K // 2:l0 + K]), wkeys + lkeys, ["w%d_1" % i])
        else:
            (vcopy if who == "v" else acopy)(row(i), win.indirect(lst[:, l0:l0 + K]), wkeys + lkeys, wk(i))

    def turn(a_in, b_in, reads):
        op("v", lambda: V.transpose(T.tt[:, 0:C], a_in), reads, ["tta"])
        op("v", lambda: V.transpose(T.tt[:, C:2 * ROW], b_in), reads + ["pads"], ["ttb"])

    def turn_row(i):
        turn(row(i), T.ww[:, ROW * i:ROW * i + C + 32], wk(i))

    def take(out, x, key, mul=None, add=float(MID)):
        win = T.tt[:, 0:2 * ROW + K].indirect(T.xl[:, 2 * x:2 * x + 2])
        rd = ["tta", "ttb", "tti", "xl%d" % x]
        if mul is None:
            ts(out[:], win, add, None, A.add, None, rd, key)
        else:
            ts(out[:], win, mul, add, A.mult, A.add, rd, key)

    def write_list(t, src, dests):
        moves = []
        for part in ([d for d in dests if not _near(T, topo, r, d)], [d for d in dests if _near(T, topo, r, d)]):
            if part:
                eng = _list_engines(T, topo, r, part[0])
                ids = [topo.addr(T.cores[d], core) for d in part]
                moves.append(RemoteDMATransfer(
                    dst_ids=[DstId(rid=a, pnc=b) for a, b in ids], dma_engine_mask=_mask(eng), remote_sem=T.sem["lst%d_%d" % (t, r)],
                    srcs=[src], dsts=[T["ll%d" % t][:, K * r:K * r + K] for _ in part]))
                note("g", "sent", len(eng), [], [])
        for call in ([moves] if t else [[m] for m in moves]):
            g.remote_dma_fused(call, local_sem=T.sem.sent)

    dma("s", "dx0", T.xt0[:, 0:4 * H], T.x[:, 0:4 * H], [], ["xt0_0"])
    dma("a", "dpr", T.pri[:], T.pr[:], [], ["pri"])
    dma("a", "du", T.ut[:], T.u[:], [], ["ut"])
    dma("s", "dx1", T.xt0[:, 4 * H:4 * C], T.x[:, 4 * H:4 * C], [], ["xt0_1"])
    op("g", lambda: g.iota(T.pi[:, 0:1], [[1, 1]], 0, 1), [], ["pi0"])
    op("g", lambda: g.iota(T.jw[:], [[0, 3], [16, K]], 0, 0, allow_small_or_imprecise_dtypes=True), [], ["jw"])
    op("g", lambda: g.iota(T.idw[:], [[1, C]], -MID, 0, allow_small_or_imprecise_dtypes=True), [], ["idw"])
    for i in range(3):
        op("v", lambda: V.memset(T.ww[:, ROW * i:ROW * i + 16], 0.0), [], ["pad%d" % i])
    op("v", lambda: V.memset(T.cc[:, 0:32], 0.0), [], ["pad5"])
    op("v", lambda: V.memset(T.cc[:, 32 + 2 * C:64 + 2 * C], 0.0), [], ["pads"])
    ts(T.pi[:, 1:2], T.pi[:, 0:1], 15, None, A.bitwise_and, None, ["pi0"], ["pi1"])
    ts(T.pi[:, 2:3], T.pi[:, 0:1], 1, None, A.bitwise_and, None, ["pi0"], ["pi2"])
    ts(T.pi[:, 3:4], T.pi[:, 0:1], 4, 1, A.logical_shift_right, A.bitwise_and, ["pi0"], ["pi3"])
    vcopy(T.pf[:, 0:4], T.pi[:, 0:4], ["pi0", "pi1", "pi2", "pi3"], ["pf"])

    def col(i):
        return T.pf[:, i:i + 1]
    op("v", lambda: V.tensor_tensor(col(4), col(2), col(3), A.not_equal), ["pf"], ["pf4"])
    ts(T.iw[:], T.jw[:, 0:K], col(1), None, A.add, None, ["jw", "pf"], ["iw"])
    ts(col(8), col(3), 15.0, 1.0, A.mult, A.add, ["pf"], ["pf8"])
    if r == 0:
        ts(col(11), col(3), -32.0, float(ROW), A.mult, A.add, ["pf"], ["pf11"])
    ts(col(5), col(4), float(ROW), None, A.mult, None, ["pf4"], ["pf5"])
    ts(col(6), col(4), float(ROW), 16.0, A.mult, A.add, ["pf4"], ["pf6"])
    ts(col(9), col(4), float(ROW), -16.0 - 2 * ROW, A.mult, A.add, ["pf4"], ["pf9"])
    if r == 0:
        ts(col(12), col(11), col(2), 16.0, A.mult, A.add, ["pf", "pf11"], ["pf12"])
    ts(T.ew[:], T.iw[:, 0:2], float(K - 1), None, A.min, None, ["iw"], ["ew"])
    ts(T.tt[:, 2 * ROW:2 * ROW + K], T.iw[:], -float(MID), None, A.add, None, ["iw"], ["tti"])
    ts(T.lq[:], T.jw[:], col(1), None, A.add, None, ["jw", "pf"], ["lq%d_%d" % (i, k) for i in range(3) for k in range(4)])
    ts(col(7), col(3), -16.0, col(6), A.mult, A.add, ["pf", "pf6"], ["pf7"])
    ts(col(10), col(9), col(3), float(2 * ROW), A.mult, A.add, ["pf", "pf9"], ["pf10"])
    ts(T.xl[:, 4:6], T.ew[:], 16.0, col(5), A.mult, A.add, ["ew", "pf5"], ["xl2"])
    if r == 0:
        ts(T.xl[:, 6:8], T.ew[:], 16.0, col(12), A.mult, A.add, ["ew", "pf12"], ["xl3"])
    ts(T.xl[:, 2:4], T.ew[:], 16.0, col(7), A.mult, A.add, ["ew", "pf7"], ["xl1"])
    ts(T.xl[:, 0:2], T.ew[:], col(8), col(10), A.mult, A.add, ["ew", "pf8", "pf10"], ["xl0"])
    vcopy(T.prw[:], T.pri[:], ["pri"], ["prw"])
    acopy(T.d1[:, 1:2 * C:2], T.idw[:], ["idw"], ["d1o"])
    ts(T.d0[:, 0:2 * C:2], T.idw[:], 0.0, None, A.mult, None, ["idw"], ["d0e"])
    op("v", lambda: V.tensor_tensor(T.d0[:, 1:2 * C:2], T.idw[:].indirect(T.prw[:]), T.d1[:, 1:2 * C:2], A.subtract), ["idw", "d1o", "prw"], ["d0o"])
    quant(T.qu, T.su, T.ut, 0, 128, ["ut"], ["qu"])
    u8, u32 = dt.uint8, dt.uint32
    dma("s", "dvc", T.qv[:].bitcast(u8), T.vc[:], ["xt0_0", "xt0_1", "ut"], ["qv"])
    dma("s", "dvs", T.sv[:], T.vs[:], [], ["sv"])
    dma("s", "dwc", T.qw[:].bitcast(u8), T.wc[:], [], ["qw"])
    dma("s", "dws", T.sw[:], T.ws[:], [], ["sw"])
    dma("s", "da", T.at[:], T.a[:], [], ["at"])

    prev, nxt = (r - 1) % N, (r + 1) % N
    halves = [(0, H), (H, C)]
    parts = [(0, CUT), (CUT, C)]
    near_prev = _near(T, topo, r, prev)
    for t in range(ROUNDS):
        arrives("dat%d" % t, sum(len(e) for e in _data_engines(T, topo, prev)), ["z%d" % t])
        for s in range(N):
            if r in _list_dests(s):
                arrives("lst%d_%d" % (t, s), len(_list_engines(T, topo, s, r)), ["ll%d_%d" % (t, s)])

    def quant_x(t, h):
        lo, hi = (parts if t else halves)[h]
        quant(T["qx%d" % t], T["sx%d" % t], T["xt%d" % t], lo, hi, ["xt%d_%d" % (t, h)], ["qx%d_%d" % (t, h)])

    def score_mm(t, h):
        lo, hi = (parts if t else halves)[h]
        for k in range(2):
            mm(4 + 2 * h + k, T.qu, T.su, 0, T["qx%d" % t], T["sx%d" % t], lo, hi, ["qu", "qx%d_%d" % (t, h)])

    for h in range(2):
        quant_x(0, h)
        score_mm(0, h)

    for t in range(ROUNDS):
        last = t == ROUNDS - 1
        xt, pl, yt, mx = T["xt%d" % t], T["pl%d" % t], T["yt%d" % t], T["mx%d" % t]
        qy, sy, qz, sz, qp, sp = [T["%s%d" % (n, t)] for n in ("qy", "sy", "qz", "sz", "qp", "sp")]
        el, es, eb, ll = T["el%d" % t], T["es%d" % t], T["eb%d" % t], T["ll%d" % t]
        xkeys = ["xt0_0", "xt0_1"] if t == 0 else ["xn%d_%d_%d" % (t - 1, h, b) for h in range(2) for b in range(4)]

        def plane(b):
            acopy(pl[:, C * b:C * b + C], xt[:, b:4 * C:4], xkeys, ["pl%d_%d" % (t, b)])

        for h, (lo, hi) in enumerate(parts if t else halves):
            acopy(T.ns[:, lo:hi], bank(5 + 2 * h, hi - lo), ["ps%d" % (5 + 2 * h)], ["ns%d" % h], scale=-1.0)
            vcopy(T.ss[:, lo:hi], bank(4 + 2 * h, hi - lo), ["ps%d" % (4 + 2 * h)], ["ss%d" % h])
        op("v", lambda: V.tensor_tensor(T.d1[:, 0:2 * C:2], T.ss[:].indirect(T.prw[:]), T.ns[:], A.is_gt),
           ["ss0", "ss1", "ns0", "ns1", "prw"], ["d1e"])
        for b in range(3):
            plane(b)
        op("v", lambda: V.tensor_tensor_scan(T.cc[:, 32:32 + 2 * C], T.d0[:], T.d1[:], 0.0, A.mult, A.add),
           ["d0e", "d0o", "d1e", "d1o"], ["cc"])
        turn(T.cc[:, 33:33 + 2 * C:2], T.cc[:, 1:2 * C + 64:2], ["cc"])
        take(T.e1, 0, ["e1"], 2.0, 2.0 * MID + 1)
        step(T.cc[:, 32:32 + 2 * C], ["cc"], T.e1, 0, ["e1"], 0)
        plane(3)
        turn_row(0)
        take(T.eq, 1, ["eq"])
        for i, d0, s0, n in ((0, 96, 64, 32), (0, 64, 32, 32), (1, 64, 0, 64), (2, 96, 0, 32), (2, 32, 0, 32)):
            vcopy(T.lq[d0:d0 + n, K * i:K * i + K], T.eq[s0:s0 + n, 0:K], ["eq"], ["lq%d_%d" % (i, k) for k in range(d0 // 32, (d0 + n) // 32)])
            if d0 == 64 and i == 0:
                step(row(0), wk(0), T.lq, 0, ["lq0_%d" % k for k in range(4)], 1)
        step(row(1), wk(1), T.lq, K, ["lq1_%d" % k for k in range(4)], 0)
        step(row(0), wk(0), T.lq, 2 * K, ["lq2_%d" % k for k in range(4)], 1)
        turn_row(1)
        elk = ["el%d_%d" % (t, k) for k in range(4)]
        esk = ["es%d_%d" % (t, k) for k in range(4)]
        dests = _list_dests(r)
        if r < 2 or not dests:
            take(T.eo, 2, ["eo"])

        def spread(buf, x, keys, between=None):
            take(buf, x, keys)
            if between:
                between()
            for k in range(3):
                vcopy(buf[32 * k:32 * k + 32, 0:K], buf[96:128, 0:K], [keys[3]], [keys[k]])
            order("g", keys, [])

        if dests:
            spread(el, 1, elk, (lambda: take(T.eo, 2, ["eo"])) if r > 1 else None)
            write_list(t, el[:, 0:K], dests if r else dests[:1])

        rid, pid = topo.addr(T.cores[nxt], core)
        deng = _data_engines(T, topo, r)
        for h, (lo, hi) in enumerate(halves):
            for b in (3, 2, 1, 0):
                src = pl[:, C * b:C * b + C].indirect(T.eo[:, lo // 16:hi // 16])
                f = acopy if b >= 2 or (b == 1 and h == 0 and dests) else vcopy
                f(yt[:, 4 * lo + b:4 * hi:4], src, ["pl%d_%d" % (t, b), "eo"], ["yt%d_%d_%d" % (t, h, b)])
            quant(qy, sy, yt, lo, hi, ["yt%d_%d_%d" % (t, h, b) for b in range(4)], ["qy%d_%d" % (t, h)])
            if len(deng) == 3 or h:
                a, e = (lo, deng[h]) if len(deng) == 3 else (0, deng[0])
                order("g", ["qy%d_%d" % (t, h)], [])
                g.remote_dma(qz[:, a:hi].bitcast(u8), qy[:, a:hi].bitcast(u8), T.sem["dat%d" % t], T.sem.sent, pid, rid, _mask(e))
                note("g", "sent", len(e), [], [])
            if r == 0 and h == 0:
                spread(es, 3, esk)
                write_list(t, es[:, 0:K], dests[1:])
        g.remote_dma(sz[:], sy[:], T.sem["dat%d" % t], T.sem.sent, pid, rid, _mask(deng[-1]))
        note("g", "sent", len(deng[-1]), [], [])
        if t == 0:
            ts(col(13), col(2), -32.0, 16.0, A.mult, A.add, ["pf"], ["pf13"])
            quant(T.qa, T.sa, T.at, 0, 128, ["at"], ["qa"])
            ts(col(14), col(13), col(3), None, A.mult, None, ["pf", "pf13"], ["pf14"])
            ts(T.xl[:, 8:10], T.ew[:], 16.0, col(14), A.mult, A.add, ["ew", "pf14"], ["xl4"])

        def pick(sq, ssc, lst, l0, lo, hi, reads, key):
            off = lst[:, l0 + lo // 16:l0 + hi // 16]
            vcopy(qp[:, lo:hi].bitcast(u32), sq[:].bitcast(u32).indirect(off), reads, ["q" + key])
            acopy(sp[:, lo:hi], ssc[:].indirect(off), reads, ["s" + key])

        xn = T["xt%d" % (t + 1)]
        zkey, bkey, pkey = "z%d" % t, "eb%d" % t, "ll%d_%d" % (t, prev)
        chain = list(range(prev - 1, -1, -1))
        state = [T.idw[:], ["idw"], 2]

        def steps(n, who):
            for _ in range(min(n, len(chain))):
                s = chain.pop(0)
                win, wkeys, i = state
                if s == r:
                    step(win, wkeys, es, 0, esk, i, who)
                else:
                    step(win, wkeys, ll, K * s, ["ll%d_%d" % (t, s)], i, who)
                state[0], state[1], state[2] = row(i), wk(i), 5 - i

        def wrap_b():
            i = 5 - state[2]
            op("v", lambda: V.transpose(T.tt[:, 0:C], row(i)), wk(i), ["tta"])
            take(eb, 4, [bkey])

        ykeys = ["qy%d_0" % t, "qy%d_1" % t]
        if t and r > 1 and near_prev:
            steps(1, "s")
        if r:
            pick(qy, sy, ll, K * prev, 0, C, ykeys + [pkey], "p%d" % t)
            for b in range(4):
                mm(b, T.qv, T.sv, 128 * b, qp, sp, 0, C, ["qv", "sv", "qp%d" % t, "sp%d" % t])
            share = near_prev or t > 0
            for b in range(4):
                (vcopy if share and b % 2 else acopy)(T.pvs[:, C * b:C * b + C], bank(b, C), ["ps%d" % b], ["pvs%d" % b, "pvt%d" % b])
        else:
            for h, (lo, hi) in enumerate(halves):
                for b in range(4):
                    mm(4 * h + b, T.qv, T.sv, 128 * b, qy, sy, lo, hi, ["qv", "sv", ykeys[h]])
                for b in range(4):
                    (vcopy if h and b % 2 else acopy)(T.pvs[:, C * b + lo:C * b + hi], bank(4 * h + b, H), ["ps%d" % (4 * h + b)],
                                                      ["pv%s%d" % ("st"[h], b)])

        def wbank(h, b):
            return 4 * (1 - h) + b

        def by_w(h, q, s, keys):
            lo, hi = parts[h]
            for b in range(4):
                mm(wbank(h, b), T.qw, T.sw, 128 * b, q, s, lo, hi, ["qw", "sw"] + keys)

        def larger(h, b):
            lo, hi = parts[h]
            k = wbank(h, b)
            op("v", lambda: V.tensor_tensor(mx[:, C * b + lo:C * b + hi], bank(k, hi - lo), T.pvs[:, C * b + lo:C * b + hi], A.max),
               ["ps%d" % k, "pvs%d" % b, "pvt%d" % b], ["mx%d_%d_%d" % (t, h, b)])

        def place(who, h, b):
            lo, hi = parts[h]
            rd = ["mx%d_%d_%d" % (t, k, b) for k in range(2)] + [bkey]
            src = mx[:, C * b:C * b + C].indirect(eb[:, lo // 16:hi // 16])
            key = ["xn%d_%d_%d" % (t, h, b)]
            if who == "a":
                acopy(xn[:, 4 * lo + b:4 * hi:4], src, rd, key, scale=SCALE)
            else:
                ts(xn[:, 4 * lo + b:4 * hi:4], src, SCALE, None, A.mult, None, rd, key)

        def after(h):
            order("v", ["xn%d_%d_%d" % (t, h, b) for b in range(4)], [])
            quant_x(t + 1, h)
            lo, hi = parts[h]
            if not last:
                score_mm(t + 1, h)
            else:
                mm(4 + h, T.qa, T.sa, 0, T["qx%d" % ROUNDS], T["sx%d" % ROUNDS], lo, hi, ["qa", "qx%d_%d" % (ROUNDS, h)])
                dma("s", "outs", T.oc[:, 4 * lo:4 * hi], T["qx%d" % ROUNDS][:, lo:hi].bitcast(u8), ["qx%d_%d" % (ROUNDS, h)], [])

        def store_lists(src, reads):
            acopy(T.ols[:], src, reads, ["ols"], bias=float(MID))
            if r < 2:
                dma("s", "outs", T.ol[:], T.ols[0:128:16, :], ["ols"], [])

        if r < 2:
            if r == 0:
                steps(N, "s")
                if last:
                    store_lists(row(1), wk(1))
                wrap_b()
                for h, (lo, hi) in enumerate(parts):
                    pick(qz, sz, eb, 0, lo, hi, [zkey, bkey], "p%d_%d" % (t, h))
                    by_w(h, qp, sp, ["qp%d_%d" % (t, h), "sp%d_%d" % (t, h)])
            else:
                if last:
                    store_lists(row(1).indirect(ll[:, K * prev:K * prev + K]), wk(1) + [pkey])
                for h in range(2):
                    by_w(h, qz, sz, [zkey])
            for h, (lo, hi) in enumerate(parts):
                for b in range(4):
                    larger(h, b)
                    acopy(xn[:, 4 * lo + b:4 * hi:4], mx[:, C * b + lo:C * b + hi], ["mx%d_%d_%d" % (t, h, b)],
                          ["xn%d_%d_%d" % (t, h, b)], scale=SCALE)
            after(0)
            after(1)
        else:
            if near_prev:
                if t:
                    steps(len(chain) - 2, "s")
                for h in range(2):
                    by_w(h, qz, sz, [zkey])
                steps(2, "a")
                for h in range(2):
                    for b in range(4):
                        larger(h, b)
            elif not t:
                steps(3, "v")
            steps(N, "s")
            if last:
                acopy(T.ow[:], row(1).indirect(ll[:, K * prev:K * prev + K]), wk(1) + [pkey], ["ow"])
            wrap_b()
            if near_prev:
                for h in range(2):
                    for b in range(4):
                        place("a" if b % 2 else "v", h, b)
                    after(h)
            else:
                for h in range(2):
                    by_w(h, qz, sz, [zkey])
                for b in range(4):
                    larger(0, b)
                    larger(1, b)
                    if b < 3:
                        place("a", 0, b)
                    if b < 2:
                        place("a", 1, b)
                place("a", 1, 2)
                for h in range(2):
                    place("v", h, 3)
                    after(h)
            if last:
                store_lists(T.ow[:].indirect(eb[:, 0:K]), ["ow", bkey])

    fk = ["qx%d_0" % ROUNDS, "qx%d_1" % ROUNDS]

    def scales(q, sem, k):
        dma(q, sem, T.osc[4 * k:4 * k + 4, :], T["sx%d" % ROUNDS][32 * k:32 * k + 4, :], fk, [])

    scales("s", "outs", 0)
    scales("s", "outs", 1)
    if r >= 2:
        dma("s", "outs", T.ol[:], T.ols[0:128:16, :], ["ols"], [])
    acopy(T.ys[:, 0:CUT], bank(4, CUT), ["ps4"], ["ys0"])
    vcopy(T.ys[:, CUT:C], bank(5, C - CUT), ["ps5"], ["ys1"])
    dma("a", "outa", T.y[:, 0:CUT], T.ys[:, 0:CUT], ["ys0"], [])
    scales("a", "outa", 2)
    scales("a", "outa", 3)
    dma("a", "outa", T.y[:, CUT:C], T.ys[:, CUT:C], ["ys1"], [])
    for sem, n in count.items():
        if waited.get(sem, 0) < n:
            g.wait_ge(T.sem[sem], n)
